import numpy as np, ml_dtypes
CORES = [40,64,80,88,96,104,120,144]
N = 8
import mx_ref
NC, G = 256, 4
C = np.float32(0.047)
BF = ml_dtypes.bfloat16
def cut(t, i, w=512):
    return t[:, w * i:w * i + w]
def tile(rs):
    return np.stack(rs, axis=2).reshape(128, -1).astype(BF)
def layer(w, X):
    out = []
    for i in range(G):
        for t in range(len(X)):
            p = mx_ref.matmul(mx_ref.quantize(cut(w, len(X) * i + t)), X[t])
            z = p if t == 0 else z + p
        out.append(z)
    return out
def masked(A, E):
    return [(e * (a > 0)) * C for a, e in zip(A, E)]
def setup_inputs(rng):
    def f(*shape):
        return mx_ref.flush((rng.standard_normal(shape, dtype=np.float32) * np.exp2(rng.integers(-2, 3, shape[:-1] + (1,)))).astype(BF))
    return {"x": f(N, 128, 512), "e": f(N, 128, 512), "a": f(N, 128, G * 512), "v": f(N, 128, 4 * NC)}
def setup_inputs_blocks(rng):
    d = setup_inputs(rng)
    for k in ("x", "e", "a", "v"): d[k] = mx_ref.spread(d[k], rng, 4)
    return d
def setup_inputs_wide(rng):
    d = setup_inputs(rng)
    for k in ("x", "e", "a", "v"): d[k] = mx_ref.flush((d[k].astype(np.float32) * np.exp2(rng.integers(-6, 7, (N, 1, 1))).astype(np.float32)).astype(BF))
    return d
def setup_inputs_zeros(rng):
    d = setup_inputs(rng); v = d["x"].reshape(N, 128, -1, 4).copy()
    v[np.broadcast_to((rng.random((N, 1, v.shape[2], 1)) < 0.33), v.shape)] = 0
    d["x"] = v.reshape(d["x"].shape)
    return d
def reference(x, e, a, v):
    T = [mx_ref.quantize(tile(masked(layer(a[j], [mx_ref.quantize(x[j])]), layer(a[j], [mx_ref.quantize(e[j])])))) for j in range(N)]
    y = np.zeros((N, 128, N * NC), np.float32)
    for r in range(N):
        qv = mx_ref.quantize(v[r])
        for j in range(N):
            y[r][:, NC * j:NC * j + NC] = mx_ref.matmul(T[j], qv)
    return {"y": y}

@@ -1,0 +1,205 @@
+from concourse.bass import DstId, RemoteDMATransfer
+from concourse.mybir import dt, AluOpType, ActivationFunctionType
+
+N, G = 8, 4
+W = 128
+NC = 256
+BANK = 512
+CONST = 0.047
+SIM_CORES = 256
+LANES = 8
+
+SCRATCH = {
+    "xt": ("sbuf", [128, 4 * W], "bfloat16"),
+    "et": ("sbuf", [128, 4 * W], "bfloat16"),
+    "at": ("sbuf", [128, 4 * W * G], "bfloat16"),
+    "vt": ("sbuf", [128, 4 * NC], "bfloat16"),
+    "qx": ("sbuf", [128, W], "float8_e4m3fn_x4"), "sx": ("sbuf", [128, W], "uint8"),
+    "qe": ("sbuf", [128, W], "float8_e4m3fn_x4"), "se": ("sbuf", [128, W], "uint8"),
+    "qa": ("sbuf", [128, W * G], "float8_e4m3fn_x4"), "sa": ("sbuf", [128, W * G], "uint8"),
+    "qv": ("sbuf", [128, NC], "float8_e4m3fn_x4"), "sv": ("sbuf", [128, NC], "uint8"),
+    "mc": ("sbuf", [128, W * G], "float32"),
+    "tt": ("sbuf", [128, 4 * W], "bfloat16"),
+    "qt": ("sbuf", [128, W * N], "float8_e4m3fn_x4"),
+    "st": ("sbuf", [128, W * N], "uint8"),
+    "ys": ("sbuf", [128, NC * N], "float32"),
+    "ps": ("psum", [128, BANK * 2 * G], "float32"),
+}
+SEMAPHORES = (["ldx", "lde", "ldv", "qx", "qe", "qv", "tt", "qt", "got", "sent", "sta", "stb"]
+              + ["%s%d" % (n, i) for n in ("lda", "qa", "u", "d", "mc") for i in range(G)]
+              + ["%s%d" % (n, i) for n in ("arr", "y", "c") for i in range(N)])
+
+
+def _plan(cores, topo):
+    lead = cores[0]
+    side_a = [c for c in cores if c == lead or topo.may_write(lead, c)]
+    side_b = [c for c in cores if c not in side_a]
+    plan = {}
+    for mine, other in ((side_a, side_b), (side_b, side_a)):
+        for i, c in enumerate(mine):
+            near = [mine[(i + 1 + s) % len(mine)] for s in range(len(mine) - 1)]
+            far = [other[(i + s) % len(other)] for s in range(len(other))]
+            owners = [h for h in range(SIM_CORES)
+                      if h != c and topo.host(h) == topo.host(c) and topo.chip(h) == topo.chip(c)
+                      and all(topo.may_write(h, d) for d in far)]
+            dies = sorted(set(topo.die(h) for h in owners), key=lambda x: x != topo.die(c))
+            per = -(-len(far) // len(dies))
+            legs = []
+            for k, die in enumerate(dies):
+                pair = [h for h in owners if topo.die(h) == die]
+                legs.append((pair[0], pair[1], far[k * per:(k + 1) * per]))
+            plan[c] = (near, legs)
+    return plan
+
+
+def _lanes(topo, src, dsts, avoid=0):
+    m = topo.mask(src, dsts[0])
+    for d in dsts[1:]:
+        m &= topo.mask(src, d)
+    m &= ~avoid
+    bits = [b for b in range(m.bit_length()) if (m >> b) & 1]
+    n = 1
+    while 2 * n <= min(len(bits), LANES):
+        n *= 2
+    mask = 0
+    for b in bits[:n]:
+        mask |= 1 << b
+    return mask, n
+
+
+def _send(g, T, topo, src, dsts, mask, sem, r, codes):
+    def view():
+        return T.qt[:, W * r:W * r + W].bitcast(dt.uint8) if codes else T.st[:, W * r:W * r + W]
+    where = []
+    for d in dsts:
+        rid, pid = topo.addr(d, src)
+        where.append(DstId(rid=rid, pnc=pid))
+    g.remote_dma_fused([RemoteDMATransfer(dst_ids=where, dma_engine_mask=mask, remote_sem=sem,
+                                          srcs=[view()], dsts=[view() for _ in dsts])], local_sem=T.sem.sent)
+
+
+def _arrivals(cores, plan, topo, me):
+    keyed = []
+    for s in cores:
+        if s == me:
+            continue
+        near, legs = plan[s]
+        if me in near:
+            keyed.append(((0, near.index(me), 0), s, 2 * _lanes(topo, s, near)[1]))
+        for k, (hc, hp, ds) in enumerate(legs):
+            if me in ds:
+                keyed.append(((1, ds.index(me), k), s, _lanes(topo, hc, ds)[1] + _lanes(topo, hp, ds)[1]))
+    return [(s, n) for _, s, n in sorted(keyed)]
+
+
+def _on_chip_lanes(topo, c, near, legs):
+    out_mask, _ = _lanes(topo, c, near)
+    codes = _lanes(topo, c, [l[0] for l in legs], avoid=out_mask)
+    plane = _lanes(topo, c, [l[1] for l in legs], avoid=codes[0])
+    return codes, plane
+
+
+def _carrier(g, core, T, topo, plan):
+    for c in T.cores:
+        near, legs = plan[c]
+        lc, lp = _on_chip_lanes(topo, c, near, legs)
+        for hc, hp, ds in legs:
+            if core in (hc, hp):
+                r = T.rank_of(c)
+                mask, n = _lanes(topo, core, ds)
+                g.wait_ge(T.sem.got, lc[1] if core == hc else lp[1])
+                _send(g, T, topo, core, ds, mask, T.sem["arr%d" % r], r, core == hc)
+                g.wait_ge(T.sem.sent, n)
+                return
+
+
+def rank_program(g, core, T, topo):
+    plan = _plan(T.cores, topo)
+    j = T.rank_of(core)
+    if j is None:
+        _carrier(g, core, T, topo, plan)
+        return
+    S = T.sem
+    V, PE, ACT, SP = g.vector, g.tensor, g.scalar, g.sync
+    near, legs = plan[core]
+
+    SP.dma_start(T.xt[:], T.x[:]).then_inc(S.ldx, 16)
+    ACT.dma_start(T.et[:], T.e[:]).then_inc(S.lde, 16)
+    for i in range(G):
+        SP.dma_start(T.at[:, 4 * W * i:4 * W * (i + 1)], T.a[:, 4 * W * i:4 * W * (i + 1)]).then_inc(S["lda%d" % i], 16)
+    SP.dma_start(T.vt[:], T.v[:]).then_inc(S.ldv, 16)
+
+    def pack_a(i):
+        V.wait_ge(S["lda%d" % i], 16)
+        V.quantize_mx(T.qa[:, W * i:W * i + W], T.sa[:, W * i:W * i + W],
+                      T.at[:, 4 * W * i:4 * W * (i + 1)]).then_inc(S["qa%d" % i], 1)
+
+    def gate(i):
+        V.wait_ge(S["u%d" % i], 1)
+        V.tensor_scalar(T.mc[:, W * i:W * i + W], T.ps[:, BANK * i:BANK * i + W], 0.0, CONST,
+                        AluOpType.is_gt, AluOpType.mult).then_inc(S["mc%d" % i], 1)
+        V.wait_ge(S["d%d" % i], 1)
+        V.wait_ge(S["mc%d" % i], 1)
+        V.tensor_tensor(T.tt[:, i:4 * W:4], T.ps[:, BANK * (G + i):BANK * (G + i) + W],
+                        T.mc[:, W * i:W * i + W], AluOpType.mult).then_inc(S.tt, 1)
+
+    V.wait_ge(S.ldx, 16)
+    V.quantize_mx(T.qx[:], T.sx[:], T.xt[:]).then_inc(S.qx, 1)
+    V.wait_ge(S.lde, 16)
+    V.quantize_mx(T.qe[:], T.se[:], T.et[:]).then_inc(S.qe, 1)
+    pack_a(0)
+    pack_a(1)
+    gate(0)
+    pack_a(2)
+    gate(1)
+    gate(2)
+    pack_a(3)
+    gate(3)
+    V.wait_ge(S.tt, G)
+    V.quantize_mx(T.qt[:, W * j:W * j + W], T.st[:, W * j:W * j + W], T.tt[:]).then_inc(S.qt, 1)
+    V.wait_ge(S.ldv, 16)
+    V.quantize_mx(T.qv[:], T.sv[:], T.vt[:]).then_inc(S.qv, 1)
+
+    PE.wait_ge(S.qx, 1)
+    PE.wait_ge(S.qe, 1)
+    for i in range(G):
+        PE.wait_ge(S["qa%d" % i], 1)
+        PE.matmul_mx(T.ps[:, BANK * i:BANK * i + W], T.qa[:, W * i:W * i + W], T.sa[:, W * i:W * i + W],
+                     T.qx[:], T.sx[:], True, True).then_inc(S["u%d" % i], 1)
+        PE.matmul_mx(T.ps[:, BANK * (G + i):BANK * (G + i) + W], T.qa[:, W * i:W * i + W], T.sa[:, W * i:W * i + W],
+                     T.qe[:], T.se[:], True, True).then_inc(S["d%d" % i], 1)
+
+    lc, lp = _on_chip_lanes(topo, core, near, legs)
+    out_mask, out_n = _lanes(topo, core, near)
+    g.wait_ge(S.qt, 1)
+    _send(g, T, topo, core, [l[0] for l in legs], lc[0], S.got, j, True)
+    _send(g, T, topo, core, [l[1] for l in legs], lp[0], S.got, j, False)
+    _send(g, T, topo, core, near, out_mask, S["arr%d" % j], j, True)
+    _send(g, T, topo, core, near, out_mask, S["arr%d" % j], j, False)
+
+    PE.wait_ge(S.qt, 1)
+    PE.wait_ge(S.qv, 1)
+    order = [(core, 0)] + _arrivals(T.cores, plan, topo, core)
+    n_sp = n_act = 0
+    for k, (s, need) in enumerate(order):
+        r = T.rank_of(s)
+        bank = T.ps[:, BANK * k:BANK * k + NC]
+        if need:
+            PE.wait_ge(S["arr%d" % r], need)
+        PE.matmul_mx(bank, T.qt[:, W * r:W * r + W], T.st[:, W * r:W * r + W],
+                     T.qv[:], T.sv[:], True, True).then_inc(S["y%d" % k], 1)
+        if k % 2 == 0:
+            V.wait_ge(S["y%d" % k], 1)
+            V.tensor_copy(T.ys[:, NC * r:NC * r + NC], bank).then_inc(S["c%d" % k], 1)
+            SP.wait_ge(S["c%d" % k], 1)
+            SP.dma_start(T.y[:, NC * r:NC * r + NC], T.ys[:, NC * r:NC * r + NC]).then_inc(S.sta, 16)
+            n_sp += 16
+        else:
+            ACT.wait_ge(S["y%d" % k], 1)
+            ACT.activation(T.ys[:, NC * r:NC * r + NC], bank, ActivationFunctionType.Copy).then_inc(S["c%d" % k], 1)
+            ACT.wait_ge(S["c%d" % k], 1)
+            ACT.dma_start(T.y[:, NC * r:NC * r + NC], T.ys[:, NC * r:NC * r + NC]).then_inc(S.stb, 16)
+            n_act += 16
+    SP.wait_ge(S.sta, n_sp)
+    ACT.wait_ge(S.stb, n_act)
+    g.wait_ge(S.sent, lc[1] + lp[1] + 2 * out_n)

@@ -18,6 +18,7 @@ SCRATCH = {
     "qe": ("sbuf", [128, W], "float8_e4m3fn_x4"), "se": ("sbuf", [128, W], "uint8"),
     "qa": ("sbuf", [128, W * G], "float8_e4m3fn_x4"), "sa": ("sbuf", [128, W * G], "uint8"),
     "qv": ("sbuf", [128, NC], "float8_e4m3fn_x4"), "sv": ("sbuf", [128, NC], "uint8"),
+    "sg": ("sbuf", [128, W * G], "float32"),
     "mc": ("sbuf", [128, W * G], "float32"),
     "tt": ("sbuf", [128, 4 * W], "bfloat16"),
     "qt": ("sbuf", [128, W * N], "float8_e4m3fn_x4"),
@@ -25,8 +26,8 @@ SCRATCH = {
     "ys": ("sbuf", [128, NC * N], "float32"),
     "ps": ("psum", [128, BANK * 2 * G], "float32"),
 }
-SEMAPHORES = (["ldx", "lde", "ldv", "qx", "qe", "qv", "tt", "qt", "got", "sent", "sta", "stb"]
-              + ["%s%d" % (n, i) for n in ("lda", "qa", "u", "d", "mc") for i in range(G)]
+SEMAPHORES = (["ldx", "lde", "ldv", "qx", "qe", "qv", "tt", "qt", "got", "sent", "sta", "stb", "yh", "ch"]
+              + ["%s%d" % (n, i) for n in ("lda", "qa", "u", "d", "sg", "mc") for i in range(G)]
               + ["%s%d" % (n, i) for n in ("arr", "y", "c") for i in range(N)])
 
 
@@ -123,51 +124,85 @@ def rank_program(g, core, T, topo):
     V, PE, ACT, SP = g.vector, g.tensor, g.scalar, g.sync
     near, legs = plan[core]
 
+    def a_cols(i):
+        return slice(4 * W * i, 4 * W * (i + 1))
+
+    def w_cols(i):
+        return slice(W * i, W * i + W)
+
+    def u_bank(i):
+        return T.ps[:, BANK * i:BANK * i + W]
+
+    def d_bank(i):
+        return T.ps[:, BANK * (G + i):BANK * (G + i) + W]
+
+    def load_a(i):
+        SP.dma_start(T.at[:, a_cols(i)], T.a[:, a_cols(i)]).then_inc(S["lda%d" % i], 16)
+
     SP.dma_start(T.xt[:], T.x[:]).then_inc(S.ldx, 16)
-    ACT.dma_start(T.et[:], T.e[:]).then_inc(S.lde, 16)
-    for i in range(G):
-        SP.dma_start(T.at[:, 4 * W * i:4 * W * (i + 1)], T.a[:, 4 * W * i:4 * W * (i + 1)]).then_inc(S["lda%d" % i], 16)
+    load_a(0)
+    SP.dma_start(T.et[:], T.e[:]).then_inc(S.lde, 16)
+    for i in range(1, G):
+        load_a(i)
     SP.dma_start(T.vt[:], T.v[:]).then_inc(S.ldv, 16)
 
     def pack_a(i):
         V.wait_ge(S["lda%d" % i], 16)
-        V.quantize_mx(T.qa[:, W * i:W * i + W], T.sa[:, W * i:W * i + W],
-                      T.at[:, 4 * W * i:4 * W * (i + 1)]).then_inc(S["qa%d" % i], 1)
-
-    def gate(i):
-        V.wait_ge(S["u%d" % i], 1)
-        V.tensor_scalar(T.mc[:, W * i:W * i + W], T.ps[:, BANK * i:BANK * i + W], 0.0, CONST,
-                        AluOpType.is_gt, AluOpType.mult).then_inc(S["mc%d" % i], 1)
-        V.wait_ge(S["d%d" % i], 1)
-        V.wait_ge(S["mc%d" % i], 1)
-        V.tensor_tensor(T.tt[:, i:4 * W:4], T.ps[:, BANK * (G + i):BANK * (G + i) + W],
-                        T.mc[:, W * i:W * i + W], AluOpType.mult).then_inc(S.tt, 1)
+        V.quantize_mx(T.qa[:, w_cols(i)], T.sa[:, w_cols(i)], T.at[:, a_cols(i)]).then_inc(S["qa%d" % i], 1)
 
     V.wait_ge(S.ldx, 16)
     V.quantize_mx(T.qx[:], T.sx[:], T.xt[:]).then_inc(S.qx, 1)
+    pack_a(0)
     V.wait_ge(S.lde, 16)
     V.quantize_mx(T.qe[:], T.se[:], T.et[:]).then_inc(S.qe, 1)
-    pack_a(0)
-    pack_a(1)
-    gate(0)
-    pack_a(2)
-    gate(1)
-    gate(2)
-    pack_a(3)
-    gate(3)
-    V.wait_ge(S.tt, G)
-    V.quantize_mx(T.qt[:, W * j:W * j + W], T.st[:, W * j:W * j + W], T.tt[:]).then_inc(S.qt, 1)
-    V.wait_ge(S.ldv, 16)
-    V.quantize_mx(T.qv[:], T.sv[:], T.vt[:]).then_inc(S.qv, 1)
+    for i in range(1, G):
+        pack_a(i)
+
+    def mm_u(i):
+        PE.matmul_mx(u_bank(i), T.qa[:, w_cols(i)], T.sa[:, w_cols(i)], T.qx[:], T.sx[:], True, True).then_inc(S["u%d" % i], 1)
+
+    def mm_d(i):
+        PE.matmul_mx(d_bank(i), T.qa[:, w_cols(i)], T.sa[:, w_cols(i)], T.qe[:], T.se[:], True, True).then_inc(S["d%d" % i], 1)
 
     PE.wait_ge(S.qx, 1)
+    PE.wait_ge(S.qa0, 1)
+    mm_u(0)
     PE.wait_ge(S.qe, 1)
-    for i in range(G):
+    mm_d(0)
+    for i in range(1, G - 2):
         PE.wait_ge(S["qa%d" % i], 1)
-        PE.matmul_mx(T.ps[:, BANK * i:BANK * i + W], T.qa[:, W * i:W * i + W], T.sa[:, W * i:W * i + W],
-                     T.qx[:], T.sx[:], True, True).then_inc(S["u%d" % i], 1)
-        PE.matmul_mx(T.ps[:, BANK * (G + i):BANK * (G + i) + W], T.qa[:, W * i:W * i + W], T.sa[:, W * i:W * i + W],
-                     T.qe[:], T.se[:], True, True).then_inc(S["d%d" % i], 1)
+        mm_u(i)
+        mm_d(i)
+    PE.wait_ge(S["qa%d" % (G - 2)], 1)
+    mm_u(G - 2)
+    PE.wait_ge(S["qa%d" % (G - 1)], 1)
+    mm_u(G - 1)
+    mm_d(G - 2)
+    mm_d(G - 1)
+
+    for i in range(G - 1):
+        ACT.wait_ge(S["u%d" % i], 1)
+        ACT.activation(T.sg[:, w_cols(i)], u_bank(i), ActivationFunctionType.Sign).then_inc(S["sg%d" % i], 1)
+        ACT.wait_ge(S["sg%d" % i], 1)
+        ACT.activation(T.mc[:, w_cols(i)], T.sg[:, w_cols(i)], ActivationFunctionType.Relu,
+                       scale=CONST).then_inc(S["mc%d" % i], 1)
+
+    def mult(i):
+        V.wait_ge(S["d%d" % i], 1)
+        V.wait_ge(S["mc%d" % i], 1)
+        V.tensor_tensor(T.tt[:, i:4 * W:4], d_bank(i), T.mc[:, w_cols(i)], AluOpType.mult).then_inc(S.tt, 1)
+
+    for i in range(G - 2):
+        mult(i)
+    V.wait_ge(S["u%d" % (G - 1)], 1)
+    V.tensor_scalar(T.mc[:, w_cols(G - 1)], u_bank(G - 1), 0.0, CONST,
+                    AluOpType.is_gt, AluOpType.mult).then_inc(S["mc%d" % (G - 1)], 1)
+    mult(G - 2)
+    mult(G - 1)
+    V.wait_ge(S.tt, G)
+    V.quantize_mx(T.qt[:, w_cols(j)], T.st[:, w_cols(j)], T.tt[:]).then_inc(S.qt, 1)
+    V.wait_ge(S.ldv, 16)
+    V.quantize_mx(T.qv[:], T.sv[:], T.vt[:]).then_inc(S.qv, 1)
 
     lc, lp = _on_chip_lanes(topo, core, near, legs)
     out_mask, out_n = _lanes(topo, core, near)
@@ -181,12 +216,31 @@ def rank_program(g, core, T, topo):
     PE.wait_ge(S.qv, 1)
     order = [(core, 0)] + _arrivals(T.cores, plan, topo, core)
     n_sp = n_act = 0
+    H = NC // 2
     for k, (s, need) in enumerate(order):
         r = T.rank_of(s)
-        bank = T.ps[:, BANK * k:BANK * k + NC]
         if need:
             PE.wait_ge(S["arr%d" % r], need)
-        PE.matmul_mx(bank, T.qt[:, W * r:W * r + W], T.st[:, W * r:W * r + W],
+        if k == len(order) - 1:
+            lo, hi = T.ps[:, BANK * k:BANK * k + H], T.ps[:, 0:H]
+            PE.matmul_mx(lo, T.qt[:, w_cols(r)], T.st[:, w_cols(r)], T.qv[:, 0:H], T.sv[:, 0:H],
+                         True, True).then_inc(S["y%d" % k], 1)
+            PE.wait_ge(S.c0, 1)
+            PE.matmul_mx(hi, T.qt[:, w_cols(r)], T.st[:, w_cols(r)], T.qv[:, H:NC], T.sv[:, H:NC],
+                         True, True).then_inc(S.yh, 1)
+            V.wait_ge(S["y%d" % k], 1)
+            V.tensor_copy(T.ys[:, NC * r:NC * r + H], lo).then_inc(S["c%d" % k], 1)
+            SP.wait_ge(S["c%d" % k], 1)
+            SP.dma_start(T.y[:, NC * r:NC * r + H], T.ys[:, NC * r:NC * r + H]).then_inc(S.sta, 16)
+            n_sp += 16
+            ACT.wait_ge(S.yh, 1)
+            ACT.activation(T.ys[:, NC * r + H:NC * r + NC], hi, ActivationFunctionType.Copy).then_inc(S.ch, 1)
+            ACT.wait_ge(S.ch, 1)
+            ACT.dma_start(T.y[:, NC * r + H:NC * r + NC], T.ys[:, NC * r + H:NC * r + NC]).then_inc(S.stb, 16)
+            n_act += 16
+            continue
+        bank = T.ps[:, BANK * k:BANK * k + NC]
+        PE.matmul_mx(bank, T.qt[:, w_cols(r)], T.st[:, w_cols(r)],
                      T.qv[:], T.sv[:], True, True).then_inc(S["y%d" % k], 1)
         if k % 2 == 0:
             V.wait_ge(S["y%d" % k], 1)

from concourse.bass import DstId, RemoteDMATransfer
from concourse.mybir import dt, AluOpType, ActivationFunctionType

N, G = 8, 4
W = 128
NC = 256
BANK = 512
CONST = 0.047
SIM_CORES = 256
LANES = 8

SCRATCH = {
    "xt": ("sbuf", [128, 4 * W], "bfloat16"),
    "et": ("sbuf", [128, 4 * W], "bfloat16"),
    "at": ("sbuf", [128, 4 * W * G], "bfloat16"),
    "vt": ("sbuf", [128, 4 * NC], "bfloat16"),
    "qx": ("sbuf", [128, W], "float8_e4m3fn_x4"), "sx": ("sbuf", [128, W], "uint8"),
    "qe": ("sbuf", [128, W], "float8_e4m3fn_x4"), "se": ("sbuf", [128, W], "uint8"),
    "qa": ("sbuf", [128, W * G], "float8_e4m3fn_x4"), "sa": ("sbuf", [128, W * G], "uint8"),
    "qv": ("sbuf", [128, NC], "float8_e4m3fn_x4"), "sv": ("sbuf", [128, NC], "uint8"),
    "sg": ("sbuf", [128, W * G], "float32"),
    "mc": ("sbuf", [128, W * G], "float32"),
    "tt": ("sbuf", [128, 4 * W], "bfloat16"),
    "qt": ("sbuf", [128, W * N], "float8_e4m3fn_x4"),
    "st": ("sbuf", [128, W * N], "uint8"),
    "ys": ("sbuf", [128, NC * N], "float32"),
    "ps": ("psum", [128, BANK * 2 * G], "float32"),
}
SEMAPHORES = (["ldx", "lde", "ldv", "qx", "qe", "qv", "tt", "qt", "got", "sent", "sta", "stb", "yh", "ch"]
              + ["%s%d" % (n, i) for n in ("lda", "qa", "u", "d", "sg", "mc") for i in range(G)]
              + ["%s%d" % (n, i) for n in ("arr", "y", "c") for i in range(N)])


def _plan(cores, topo):
    lead = cores[0]
    side_a = [c for c in cores if c == lead or topo.may_write(lead, c)]
    side_b = [c for c in cores if c not in side_a]
    plan = {}
    for mine, other in ((side_a, side_b), (side_b, side_a)):
        for i, c in enumerate(mine):
            near = [mine[(i + 1 + s) % len(mine)] for s in range(len(mine) - 1)]
            far = [other[(i + s) % len(other)] for s in range(len(other))]
            owners = [h for h in range(SIM_CORES)
                      if h != c and topo.host(h) == topo.host(c) and topo.chip(h) == topo.chip(c)
                      and all(topo.may_write(h, d) for d in far)]
            dies = sorted(set(topo.die(h) for h in owners), key=lambda x: x != topo.die(c))
            per = -(-len(far) // len(dies))
            legs = []
            for k, die in enumerate(dies):
                pair = [h for h in owners if topo.die(h) == die]
                legs.append((pair[0], pair[1], far[k * per:(k + 1) * per]))
            plan[c] = (near, legs)
    return plan


def _lanes(topo, src, dsts, avoid=0):
    m = topo.mask(src, dsts[0])
    for d in dsts[1:]:
        m &= topo.mask(src, d)
    m &= ~avoid
    bits = [b for b in range(m.bit_length()) if (m >> b) & 1]
    n = 1
    while 2 * n <= min(len(bits), LANES):
        n *= 2
    mask = 0
    for b in bits[:n]:
        mask |= 1 << b
    return mask, n


def _send(g, T, topo, src, dsts, mask, sem, r, codes):
    def view():
        return T.qt[:, W * r:W * r + W].bitcast(dt.uint8) if codes else T.st[:, W * r:W * r + W]
    where = []
    for d in dsts:
        rid, pid = topo.addr(d, src)
        where.append(DstId(rid=rid, pnc=pid))
    g.remote_dma_fused([RemoteDMATransfer(dst_ids=where, dma_engine_mask=mask, remote_sem=sem,
                                          srcs=[view()], dsts=[view() for _ in dsts])], local_sem=T.sem.sent)


def _arrivals(cores, plan, topo, me):
    keyed = []
    for s in cores:
        if s == me:
            continue
        near, legs = plan[s]
        if me in near:
            keyed.append(((0, near.index(me), 0), s, 2 * _lanes(topo, s, near)[1]))
        for k, (hc, hp, ds) in enumerate(legs):
            if me in ds:
                keyed.append(((1, ds.index(me), k), s, _lanes(topo, hc, ds)[1] + _lanes(topo, hp, ds)[1]))
    return [(s, n) for _, s, n in sorted(keyed)]


def _on_chip_lanes(topo, c, near, legs):
    out_mask, _ = _lanes(topo, c, near)
    codes = _lanes(topo, c, [l[0] for l in legs], avoid=out_mask)
    plane = _lanes(topo, c, [l[1] for l in legs], avoid=codes[0])
    return codes, plane


def _carrier(g, core, T, topo, plan):
    for c in T.cores:
        near, legs = plan[c]
        lc, lp = _on_chip_lanes(topo, c, near, legs)
        for hc, hp, ds in legs:
            if core in (hc, hp):
                r = T.rank_of(c)
                mask, n = _lanes(topo, core, ds)
                g.wait_ge(T.sem.got, lc[1] if core == hc else lp[1])
                _send(g, T, topo, core, ds, mask, T.sem["arr%d" % r], r, core == hc)
                g.wait_ge(T.sem.sent, n)
                return


def rank_program(g, core, T, topo):
    plan = _plan(T.cores, topo)
    j = T.rank_of(core)
    if j is None:
        _carrier(g, core, T, topo, plan)
        return
    S = T.sem
    V, PE, ACT, SP = g.vector, g.tensor, g.scalar, g.sync
    near, legs = plan[core]

    def a_cols(i):
        return slice(4 * W * i, 4 * W * (i + 1))

    def w_cols(i):
        return slice(W * i, W * i + W)

    def u_bank(i):
        return T.ps[:, BANK * i:BANK * i + W]

    def d_bank(i):
        return T.ps[:, BANK * (G + i):BANK * (G + i) + W]

    def load_a(i):
        SP.dma_start(T.at[:, a_cols(i)], T.a[:, a_cols(i)]).then_inc(S["lda%d" % i], 16)

    SP.dma_start(T.xt[:], T.x[:]).then_inc(S.ldx, 16)
    load_a(0)
    SP.dma_start(T.et[:], T.e[:]).then_inc(S.lde, 16)
    for i in range(1, G):
        load_a(i)
    SP.dma_start(T.vt[:], T.v[:]).then_inc(S.ldv, 16)

    def pack_a(i):
        V.wait_ge(S["lda%d" % i], 16)
        V.quantize_mx(T.qa[:, w_cols(i)], T.sa[:, w_cols(i)], T.at[:, a_cols(i)]).then_inc(S["qa%d" % i], 1)

    V.wait_ge(S.ldx, 16)
    V.quantize_mx(T.qx[:], T.sx[:], T.xt[:]).then_inc(S.qx, 1)
    pack_a(0)
    V.wait_ge(S.lde, 16)
    V.quantize_mx(T.qe[:], T.se[:], T.et[:]).then_inc(S.qe, 1)
    for i in range(1, G):
        pack_a(i)

    def mm_u(i):
        PE.matmul_mx(u_bank(i), T.qa[:, w_cols(i)], T.sa[:, w_cols(i)], T.qx[:], T.sx[:], True, True).then_inc(S["u%d" % i], 1)

    def mm_d(i):
        PE.matmul_mx(d_bank(i), T.qa[:, w_cols(i)], T.sa[:, w_cols(i)], T.qe[:], T.se[:], True, True).then_inc(S["d%d" % i], 1)

    PE.wait_ge(S.qx, 1)
    PE.wait_ge(S.qa0, 1)
    mm_u(0)
    PE.wait_ge(S.qe, 1)
    mm_d(0)
    for i in range(1, G - 2):
        PE.wait_ge(S["qa%d" % i], 1)
        mm_u(i)
        mm_d(i)
    PE.wait_ge(S["qa%d" % (G - 2)], 1)
    mm_u(G - 2)
    PE.wait_ge(S["qa%d" % (G - 1)], 1)
    mm_u(G - 1)
    mm_d(G - 2)
    mm_d(G - 1)

    for i in range(G - 1):
        ACT.wait_ge(S["u%d" % i], 1)
        ACT.activation(T.sg[:, w_cols(i)], u_bank(i), ActivationFunctionType.Sign).then_inc(S["sg%d" % i], 1)
        ACT.wait_ge(S["sg%d" % i], 1)
        ACT.activation(T.mc[:, w_cols(i)], T.sg[:, w_cols(i)], ActivationFunctionType.Relu,
                       scale=CONST).then_inc(S["mc%d" % i], 1)

    def mult(i):
        V.wait_ge(S["d%d" % i], 1)
        V.wait_ge(S["mc%d" % i], 1)
        V.tensor_tensor(T.tt[:, i:4 * W:4], d_bank(i), T.mc[:, w_cols(i)], AluOpType.mult).then_inc(S.tt, 1)

    for i in range(G - 2):
        mult(i)
    V.wait_ge(S["u%d" % (G - 1)], 1)
    V.tensor_scalar(T.mc[:, w_cols(G - 1)], u_bank(G - 1), 0.0, CONST,
                    AluOpType.is_gt, AluOpType.mult).then_inc(S["mc%d" % (G - 1)], 1)
    mult(G - 2)
    mult(G - 1)
    V.wait_ge(S.tt, G)
    V.quantize_mx(T.qt[:, w_cols(j)], T.st[:, w_cols(j)], T.tt[:]).then_inc(S.qt, 1)
    V.wait_ge(S.ldv, 16)
    V.quantize_mx(T.qv[:], T.sv[:], T.vt[:]).then_inc(S.qv, 1)

    lc, lp = _on_chip_lanes(topo, core, near, legs)
    out_mask, out_n = _lanes(topo, core, near)
    g.wait_ge(S.qt, 1)
    _send(g, T, topo, core, [l[0] for l in legs], lc[0], S.got, j, True)
    _send(g, T, topo, core, [l[1] for l in legs], lp[0], S.got, j, False)
    _send(g, T, topo, core, near, out_mask, S["arr%d" % j], j, True)
    _send(g, T, topo, core, near, out_mask, S["arr%d" % j], j, False)

    PE.wait_ge(S.qt, 1)
    PE.wait_ge(S.qv, 1)
    order = [(core, 0)] + _arrivals(T.cores, plan, topo, core)
    n_sp = n_act = 0
    H = NC // 2
    for k, (s, need) in enumerate(order):
        r = T.rank_of(s)
        if need:
            PE.wait_ge(S["arr%d" % r], need)
        if k == len(order) - 1:
            lo, hi = T.ps[:, BANK * k:BANK * k + H], T.ps[:, 0:H]
            PE.matmul_mx(lo, T.qt[:, w_cols(r)], T.st[:, w_cols(r)], T.qv[:, 0:H], T.sv[:, 0:H],
                         True, True).then_inc(S["y%d" % k], 1)
            PE.wait_ge(S.c0, 1)
            PE.matmul_mx(hi, T.qt[:, w_cols(r)], T.st[:, w_cols(r)], T.qv[:, H:NC], T.sv[:, H:NC],
                         True, True).then_inc(S.yh, 1)
            V.wait_ge(S["y%d" % k], 1)
            V.tensor_copy(T.ys[:, NC * r:NC * r + H], lo).then_inc(S["c%d" % k], 1)
            SP.wait_ge(S["c%d" % k], 1)
            SP.dma_start(T.y[:, NC * r:NC * r + H], T.ys[:, NC * r:NC * r + H]).then_inc(S.sta, 16)
            n_sp += 16
            ACT.wait_ge(S.yh, 1)
            ACT.activation(T.ys[:, NC * r + H:NC * r + NC], hi, ActivationFunctionType.Copy).then_inc(S.ch, 1)
            ACT.wait_ge(S.ch, 1)
            ACT.dma_start(T.y[:, NC * r + H:NC * r + NC], T.ys[:, NC * r + H:NC * r + NC]).then_inc(S.stb, 16)
            n_act += 16
            continue
        bank = T.ps[:, BANK * k:BANK * k + NC]
        PE.matmul_mx(bank, T.qt[:, w_cols(r)], T.st[:, w_cols(r)],
                     T.qv[:], T.sv[:], True, True).then_inc(S["y%d" % k], 1)
        if k % 2 == 0:
            V.wait_ge(S["y%d" % k], 1)
            V.tensor_copy(T.ys[:, NC * r:NC * r + NC], bank).then_inc(S["c%d" % k], 1)
            SP.wait_ge(S["c%d" % k], 1)
            SP.dma_start(T.y[:, NC * r:NC * r + NC], T.ys[:, NC * r:NC * r + NC]).then_inc(S.sta, 16)
            n_sp += 16
        else:
            ACT.wait_ge(S["y%d" % k], 1)
            ACT.activation(T.ys[:, NC * r:NC * r + NC], bank, ActivationFunctionType.Copy).then_inc(S["c%d" % k], 1)
            ACT.wait_ge(S["c%d" % k], 1)
            ACT.dma_start(T.y[:, NC * r:NC * r + NC], T.ys[:, NC * r:NC * r + NC]).then_inc(S.stb, 16)
            n_act += 16
    SP.wait_ge(S.sta, n_sp)
    ACT.wait_ge(S.stb, n_act)
    g.wait_ge(S.sent, lc[1] + lp[1] + 2 * out_n)
